import numpy as np
import ml_dtypes


def mxq(x, axis, fmt="e4m3"):
    dtype, down = {"e4m3": (ml_dtypes.float8_e4m3fn, 7), "e5m2": (ml_dtypes.float8_e5m2, 14)}[fmt]
    v = np.moveaxis(np.asarray(x, np.float32).astype(ml_dtypes.bfloat16).astype(np.float64), axis, -1)
    blocks = v.reshape(v.shape[:-1] + (-1, 32))
    amax = np.abs(blocks).max(-1, keepdims=True)
    byte = np.maximum(np.where(amax > 0, np.frexp(amax)[1] - 1 + 127, 0) - down, 1)
    scale = np.exp2(byte - 127.0)
    codes = (blocks / scale).astype(np.float32).astype(dtype).astype(np.float64)
    return np.moveaxis((codes * scale).reshape(v.shape), -1, axis)


WIDE = False


def mx_kscale(k):
    if not WIDE:
        return np.ones(k)
    levels = np.array([18, -18])
    if k % 512:
        return np.exp2(np.random.permutation(np.resize(levels, k // 32))).repeat(32)
    a = np.empty((k // 512, 16))
    for p in range(k // 512):
        a[p, :8] = np.random.permutation(np.resize(levels, 8))
        for g in range(8):
            far = levels[np.abs(levels - a[p, g]) >= 10]
            a[p, g + 8] = far[np.random.randint(len(far))]
    return np.exp2(a.ravel()).repeat(32)


def f64(x):
    return np.asarray(x).astype(np.float64)


def striped(idx):
    return np.tile(np.asarray(idx).reshape(-1, 16).T, (8, 1)).astype(np.uint16)


def unstriped(offs):
    return offs[:16].T.reshape(-1).astype(np.int64)


E2M1 = np.array([0.0, 0.5, 1.0, 1.5, 2.0, 3.0, 4.0, 6.0, -0.0, -0.5, -1.0, -1.5, -2.0, -3.0, -4.0, -6.0])


def pack_weight(w, fmt):
    k, n = w.shape
    w = f64(np.asarray(w, np.float32).astype(ml_dtypes.bfloat16)).reshape(k // 32, 32, n)
    amax = np.abs(w).max(1)
    if fmt == "e4m3":
        byte = np.frexp(amax)[1] - 1 + 127 - 7
    else:
        mant, ex = np.frexp(amax / 6.0)
        byte = np.where(mant > 0.5, ex, ex - 1) + 127
    byte = np.clip(np.where(amax > 0, byte, 1), 1, 254)
    scaled = (w * np.exp2(127.0 - byte)[:, None, :]).reshape(k, n).astype(np.float32)
    by_word = np.ascontiguousarray(scaled.reshape(k // 512, 128, 4, n).transpose(0, 1, 3, 2))
    if fmt == "e4m3":
        words = by_word.astype(ml_dtypes.float8_e4m3fn).view(np.uint8)
    else:
        c = by_word.astype(ml_dtypes.float4_e2m1fn).view(np.uint8) & 0xF
        words = (c[..., 0::2] | (c[..., 1::2] << 4)).reshape(k // 512, 128, 2 * n)
    return np.ascontiguousarray(words), np.ascontiguousarray(byte.astype(np.uint8).reshape(k // 512, 16, n))


def unpack_weight(words, scales, fmt):
    g, _, n = scales.shape
    words = np.ascontiguousarray(words).reshape(g, 128, n, -1)
    if fmt == "e4m3":
        vals = words.view(ml_dtypes.float8_e4m3fn).astype(np.float64)
    else:
        nib = np.empty((g, 128, n, 4), np.uint8)
        nib[..., 0::2] = words & 0xF
        nib[..., 1::2] = words >> 4
        vals = E2M1[nib]
    vals = vals * np.repeat(np.exp2(scales.astype(np.float64) - 127.0), 8, axis=1)[..., None]
    return vals.transpose(0, 1, 3, 2).reshape(g * 512, n)


B, N, T, D, R = 1, 512, 2048, 512, 1024


def setup_inputs():
    n = np.random.standard_normal
    idx = np.random.permutation(T)[:B * N]
    s = mx_kscale(D)[:, None]
    z = mx_kscale(R)[:, None]
    x = n((B, D, R))
    vp = pack_weight(n((D, T)) / np.sqrt(D) / s, "e4m3")
    return {
        "xT": (x * s).astype(np.float32),
        "wT": (n((D, T)) * (1.00 / np.sqrt(D)) / s).astype(np.float32),
        "v_words": vp[0],
        "v_scales": vp[1],
        "wt": (np.random.uniform(0.5, 1.5, (B, R, 1)) * 1.0 / np.sqrt(R) * z).astype(np.float32),
        "xm": (x.transpose(0, 2, 1) / z).astype(np.float32),
        "offs": striped(idx),
    }


def reference(xT, wT, v_words, v_scales, wt, xm, offs):
    idx = unstriped(offs)
    v = unpack_weight(v_words, v_scales, "e4m3")
    pick = lambda x: x[:, idx].reshape(x.shape[0], B, N).transpose(1, 0, 2)
    xq = mxq(f64(xT), 1, "e4m3").transpose(0, 2, 1)
    a = xq @ mxq(pick(f64(wT)), 1, "e4m3")
    av = xq @ pick(v)
    g = f64(wt) * np.minimum(np.maximum(a - av, -1.0), 1.0)
    dw = mxq(f64(xm), 1, "e4m3").transpose(0, 2, 1) @ mxq(g, 1, "e5m2")
    gw = np.zeros((D, T))
    gw[:, idx] = dw.transpose(1, 0, 2).reshape(D, B * N)
    return gw

@@ -1,0 +1,227 @@
+from contextlib import ExitStack
+
+import concourse.mybir as mybir
+
+N, T, D, R = 512, 2048, 512, 1024
+FLOPS = 3 * 2 * N * D * R
+
+F32 = mybir.dt.float32
+BF16 = mybir.dt.bfloat16
+I32 = mybir.dt.int32
+U32 = mybir.dt.uint32
+U16 = mybir.dt.uint16
+U8 = mybir.dt.uint8
+E4M3 = mybir.dt.float8_e4m3fn_x4
+E5M2 = mybir.dt.float8_e5m2_x4
+ALU = mybir.AluOpType
+COPY = mybir.ActivationFunctionType.Copy
+
+P = 128
+PACK = 4
+K_PASS = P * PACK
+ROW_PASSES = R // K_PASS
+D_TILES = D // P
+HALF = N // 2
+
+W_SLOTS_ON_SCALAR = 192
+X_COLUMNS_ON_SCALAR = 40
+
+
+def woven(ap):
+    return ap.rearrange("p (c i) t -> p c t i", i=4)
+
+
+def planar(ap):
+    return ap.rearrange("p t (c i) -> p c t i", i=4)
+
+
+def tile_attend_gds_hub_kernel(tc, xT, wT, v_words, v_scales, wt, xm, offs, out):
+    nc = tc.nc
+    with ExitStack() as ctx:
+        keep = ctx.enter_context(tc.tile_pool(name="keep", bufs=1))
+        score_psum = ctx.enter_context(tc.psum_pool(name="score_psum", bufs=1))
+        grad_psum = ctx.enter_context(tc.psum_pool(name="grad_psum", bufs=2))
+
+        def tile(shape, dtype, name, reuses=None):
+            return keep.tile(shape, dtype, name=name, tag=reuses or name, align_bytes=64)
+
+        offsets = tile([P, N // 16], U16, "offsets")
+        nc.sync.dma_start(offsets[:], offs)
+        v_scale_table = tile([P, T], U8, "v_scale_table")
+        nc.gpsimd.memset(v_scale_table[:].bitcast(I32), 0)
+
+        w_planes = [tile([P, T], F32, "w_plane%d" % j) for j in range(PACK)]
+        w_rows = wT.rearrange("(p j) c -> p j c", j=PACK)
+        weight = tile([P, ROW_PASSES, PACK], F32, "weight")
+        nc.sync.dma_start(w_planes[0][:], w_rows[:, 0, :])
+        nc.sync.dma_start(weight[:], wt[0].rearrange("(g p t) o -> p g (t o)", p=P, t=PACK))
+        nc.sync.dma_start(w_planes[1][:], w_rows[:, 1, :])
+        for q in range(4):
+            nc.sync.dma_start(
+                v_scale_table[32 * q : 32 * q + 4, :].bitcast(I32),
+                v_scales[0, 4 * q : 4 * q + 4, :].bitcast(I32),
+            )
+        for j in range(2, PACK):
+            nc.sync.dma_start(w_planes[j][:], w_rows[:, j, :])
+
+        x_rows = xT[0].rearrange("(p j) r -> p j r", j=PACK)
+        x_first = tile([P, PACK, K_PASS], F32, "x_first")
+        nc.sync.dma_start(x_first[:], x_rows[:, :, 0:K_PASS])
+        v_word_table = tile([P, T], U32, "v_word_table")
+        nc.sync.dma_start(v_word_table[:].bitcast(I32), v_words[0].rearrange("p c j -> p (c j)").bitcast(I32))
+        x_second = [tile([P, PACK, K_PASS // 2], F32, "x_second%d" % h) for h in range(2)]
+        for h in range(2):
+            r0 = K_PASS + h * (K_PASS // 2)
+            nc.sync.dma_start(x_second[h][:], x_rows[:, :, r0 : r0 + K_PASS // 2])
+        m_raw = [tile([P, PACK, D], F32, "m_raw%d" % g) for g in range(ROW_PASSES)]
+        m_rows = xm[0].rearrange("(g p t) d -> g p t d", p=P, t=PACK)
+        for g in range(ROW_PASSES):
+            nc.sync.dma_start(m_raw[g][:], m_rows[g])
+
+        windows = [tile([P, T], F32, "window%d" % k) for k in range(D_TILES)]
+        for k in range(D_TILES):
+            (nc.vector if k < 2 else nc.gpsimd).memset(windows[k][:].bitcast(I32), 0)
+
+        neg_weight = tile([P, ROW_PASSES, PACK], F32, "neg_weight")
+        upper = tile([P, ROW_PASSES, PACK], F32, "upper")
+        lower = tile([P, ROW_PASSES, PACK], F32, "lower")
+        nc.scalar.activation(neg_weight[:], weight[:], COPY, scale=-1.0)
+        nc.vector.tensor_tensor(upper[:], weight[:], neg_weight[:], ALU.max)
+        nc.vector.tensor_tensor(lower[:], weight[:], neg_weight[:], ALU.min)
+
+        w_picked = tile([P, PACK, N], F32, "w_picked")
+        v_scale = tile([P, N], U8, "v_scale")
+        for j in range(PACK):
+            nc.vector.tensor_copy(w_picked[:, j, :], w_planes[j][:].indirect(offsets[:]))
+            if j == PACK - 2:
+                nc.vector.tensor_copy(v_scale[:], v_scale_table[:].indirect(offsets[:]))
+
+        w_neg = tile([P, N, PACK], BF16, "w_neg")
+        s = W_SLOTS_ON_SCALAR
+        nc.scalar.activation(woven(w_neg[:, 0:s, :]), planar(w_picked[:, :, 0:s]), COPY, scale=-1.0)
+        nc.vector.tensor_scalar(woven(w_neg[:, s:N, :]), planar(w_picked[:, :, s:N]), -1.0, None, ALU.mult)
+        w_codes = tile([P, N], U32, "w_codes")
+        w_scale = tile([P, N], U8, "w_scale")
+        nc.vector.quantize_mx(w_codes[:].bitcast(E4M3), w_scale[:], w_neg[:].rearrange("p c t -> p (c t)"))
+
+        x_codes = [tile([P, K_PASS], U32, "x_codes%d" % g) for g in range(ROW_PASSES)]
+        x_scale = [tile([P, K_PASS], U8, "x_scale%d" % g) for g in range(ROW_PASSES)]
+
+        def by_row(ap):
+            return ap.rearrange("p j (m t) -> p m j t", t=PACK)
+
+        def score_pass(bank, g, t, codes, scale, first):
+            cols = slice(t * P, (t + 1) * P)
+            nc.tensor.matmul_mx(
+                bank[:],
+                lhsT=x_codes[g][:, cols].bitcast(E4M3),
+                lhsT_scale=x_scale[g][:, cols],
+                rhs=codes[:].bitcast(E4M3),
+                rhs_scale=scale[:],
+                start=first,
+                stop=not first,
+            )
+
+        g_planes = []
+        g_codes = [tile([P, N], U32, "g_codes%d" % g) for g in range(ROW_PASSES)]
+        g_scale = [tile([P, N], U8, "g_scale%d" % g) for g in range(ROW_PASSES)]
+
+        def weigh_and_clip(bank, g, t):
+            weighted = tile([P, N], F32, "weighted%d_%d" % (g, t))
+            nc.scalar.activation(weighted[:], bank[:], COPY, scale=neg_weight[:, g, t : t + 1])
+            nc.vector.tensor_scalar(
+                g_planes[g][:, t, :], weighted[:], lower[:, g, t : t + 1], upper[:, g, t : t + 1], ALU.max, ALU.min
+            )
+
+        def quantize_g(g, slots, source):
+            nc.vector.quantize_mx(
+                g_codes[g][:, slots].bitcast(E5M2), g_scale[g][:, slots], source[:].rearrange("p c t -> p (c t)")
+            )
+
+        m_codes = [tile([P, ROW_PASSES * P], U32, "m_codes%d" % k) for k in range(D_TILES)]
+        m_scale = [tile([P, ROW_PASSES * P], U8, "m_scale%d" % k) for k in range(D_TILES)]
+
+        def weave_m(k, reuses):
+            m_woven = tile([P, ROW_PASSES, P, PACK], BF16, "m_woven%d" % k, reuses)
+            for g in range(ROW_PASSES):
+                nc.scalar.copy(woven(m_woven[:, g]), planar(m_raw[g][:, :, k * P : (k + 1) * P]))
+            return m_woven
+
+        def quantize_m(k, m_woven):
+            nc.vector.quantize_mx(m_codes[k][:].bitcast(E4M3), m_scale[k][:], m_woven[:].rearrange("p g c t -> p (g c t)"))
+
+        def gradient_passes(k):
+            bank = grad_psum.tile([P, N], F32, name="grad_bank")
+            for g in reversed(range(ROW_PASSES)):
+                cols = slice(g * P, (g + 1) * P)
+                nc.tensor.matmul_mx(
+                    bank[:],
+                    lhsT=m_codes[k][:, cols].bitcast(E4M3),
+                    lhsT_scale=m_scale[k][:, cols],
+                    rhs=g_codes[g][:].bitcast(E5M2),
+                    rhs_scale=g_scale[g][:],
+                    start=(g == ROW_PASSES - 1),
+                    stop=(g == 0),
+                )
+            return bank
+
+        x_dealt = tile([P, PACK, P, PACK], BF16, "x_dealt0", "w_plane3")
+        dst = x_dealt[:].rearrange("p t m j -> p m j t")
+        h = X_COLUMNS_ON_SCALAR
+        nc.scalar.copy(dst[:, 0:h], by_row(x_first[:])[:, 0:h])
+        nc.vector.tensor_copy(dst[:, h:P], by_row(x_first[:])[:, h:P])
+        nc.vector.quantize_mx(x_codes[0][:].bitcast(E4M3), x_scale[0][:], x_dealt[:].rearrange("p t m j -> p (t m j)"))
+
+        v_codes = tile([P, N], U32, "v_codes", "w_plane3")
+        nc.vector.tensor_copy(v_codes[:], v_word_table[:].indirect(offsets[:]))
+
+        x_dealt = tile([P, PACK, P, PACK], BF16, "x_dealt1", "v_word_table")
+        dst = x_dealt[:].rearrange("p t m j -> p m j t")
+        for h in range(2):
+            nc.vector.tensor_copy(dst[:, h * (P // 2) : (h + 1) * (P // 2)], by_row(x_second[h][:]))
+        for t in range(PACK):
+            cols = slice(t * P, (t + 1) * P)
+            nc.vector.quantize_mx(
+                x_codes[1][:, cols].bitcast(E4M3), x_scale[1][:, cols], x_dealt[:, t].rearrange("p m j -> p (m j)")
+            )
+        g_planes.append(tile([P, PACK, N], BF16, "g_planes0", "v_word_table"))
+        g_planes.append(tile([P, PACK, N], BF16, "g_planes1"))
+        for pair in range(0, PACK, 2):
+            banks = [score_psum.tile([P, N], F32, name="first_bank%d" % i) for i in range(2)]
+            for i in range(2):
+                score_pass(banks[i], 0, pair + i, w_codes, w_scale, True)
+            for i in range(2):
+                score_pass(banks[i], 0, pair + i, v_codes, v_scale, False)
+            for i in range(2):
+                weigh_and_clip(banks[i], 0, pair + i)
+        g_first_low = tile([P, HALF, PACK], BF16, "g_first_low")
+        nc.vector.tensor_copy(woven(g_first_low[:]), planar(g_planes[0][:, :, 0:HALF]))
+
+        for t in range(PACK):
+            bank = score_psum.tile([P, N], F32, name="second_bank%d" % t)
+            score_pass(bank, 1, t, w_codes, w_scale, True)
+            score_pass(bank, 1, t, v_codes, v_scale, False)
+            weigh_and_clip(bank, 1, t)
+            if t == 0:
+                quantize_g(0, slice(0, HALF), g_first_low)
+
+        g_second = tile([P, N, PACK], BF16, "g_second")
+        nc.vector.tensor_copy(woven(g_second[:]), planar(g_planes[1][:]))
+        m_woven = weave_m(0, "x_codes1")
+        g_first_high = tile([P, HALF, PACK], BF16, "g_first_high", "neg_weight")
+        nc.scalar.copy(woven(g_first_high[:]), planar(g_planes[0][:, :, HALF:N]))
+        quantize_m(0, m_woven)
+        quantize_g(1, slice(0, N), g_second)
+        quantize_g(0, slice(HALF, N), g_first_high)
+
+        m_woven = weave_m(1, "g_planes1")
+        quantize_m(1, m_woven)
+        for k in range(D_TILES):
+            bank = gradient_passes(k)
+            if 1 <= k < D_TILES - 1:
+                m_woven = weave_m(k + 1, "m_codes%d" % (k - 1))
+                quantize_m(k + 1, m_woven)
+            grad = tile([P, N], F32, "grad%d" % k)
+            nc.scalar.copy(grad[:], bank[:])
+            nc.vector.tensor_copy(windows[k][:].indirect(offsets[:]), grad[:])
+            nc.sync.dma_start(out[k * P : (k + 1) * P, :], windows[k][:])

@@ -15,6 +15,7 @@ E4M3 = mybir.dt.float8_e4m3fn_x4
 E5M2 = mybir.dt.float8_e5m2_x4
 ALU = mybir.AluOpType
 COPY = mybir.ActivationFunctionType.Copy
+ABS = mybir.ActivationFunctionType.Abs
 
 P = 128
 PACK = 4
@@ -23,8 +24,9 @@ ROW_PASSES = R // K_PASS
 D_TILES = D // P
 HALF = N // 2
 
-W_SLOTS_ON_SCALAR = 192
+W_SLOTS_ON_SCALAR = 224
 X_COLUMNS_ON_SCALAR = 40
+WINDOWS_ON_VECTOR = 2
 
 
 def woven(ap):
@@ -33,6 +35,14 @@ def woven(ap):
 
 def planar(ap):
     return ap.rearrange("p t (c i) -> p c t i", i=4)
+
+
+def by_row(ap):
+    return ap.rearrange("p j (m t) -> p m j t", t=PACK)
+
+
+def dealt(ap):
+    return ap.rearrange("p t m j -> p m j t")
 
 
 def tile_attend_gds_hub_kernel(tc, xT, wT, v_words, v_scales, wt, xm, offs, out):
@@ -46,48 +56,35 @@ def tile_attend_gds_hub_kernel(tc, xT, wT, v_words, v_scales, wt, xm, offs, out)
             return keep.tile(shape, dtype, name=name, tag=reuses or name, align_bytes=64)
 
         offsets = tile([P, N // 16], U16, "offsets")
-        nc.sync.dma_start(offsets[:], offs)
+
+        weight = tile([P, ROW_PASSES, PACK], F32, "weight")
+        nc.scalar.dma_start(weight[:], wt[0].rearrange("(g p t) o -> p g (t o)", p=P, t=PACK))
+        neg_weight = tile([P, ROW_PASSES, PACK], F32, "neg_weight")
+        upper = tile([P, ROW_PASSES, PACK], F32, "upper")
+        lower = tile([P, ROW_PASSES, PACK], F32, "lower")
+        nc.scalar.activation(neg_weight[:], weight[:], COPY, scale=-1.0)
+        nc.scalar.activation(upper[:], weight[:], ABS)
+        nc.scalar.activation(lower[:], upper[:], COPY, scale=-1.0)
+
         v_scale_table = tile([P, T], U8, "v_scale_table")
         nc.gpsimd.memset(v_scale_table[:].bitcast(I32), 0)
+        windows = [tile([P, T], F32, "window%d" % k) for k in range(D_TILES)]
+        for k in range(D_TILES):
+            (nc.vector if k < WINDOWS_ON_VECTOR else nc.gpsimd).memset(windows[k][:].bitcast(I32), 0)
 
-        w_planes = [tile([P, T], F32, "w_plane%d" % j) for j in range(PACK)]
+        w_planes = [tile([P, T], F32, "w_plane%d" % j) for j in range(PACK - 1)]
+        w_planes.append(tile([P, T], F32, "w_plane3", "weight"))
         w_rows = wT.rearrange("(p j) c -> p j c", j=PACK)
-        weight = tile([P, ROW_PASSES, PACK], F32, "weight")
-        nc.sync.dma_start(w_planes[0][:], w_rows[:, 0, :])
-        nc.sync.dma_start(weight[:], wt[0].rearrange("(g p t) o -> p g (t o)", p=P, t=PACK))
-        nc.sync.dma_start(w_planes[1][:], w_rows[:, 1, :])
+        for j in range(PACK - 1):
+            nc.sync.dma_start(w_planes[j][:], w_rows[:, j, :])
+            if j == 0:
+                nc.sync.dma_start(offsets[:], offs)
         for q in range(4):
             nc.sync.dma_start(
                 v_scale_table[32 * q : 32 * q + 4, :].bitcast(I32),
                 v_scales[0, 4 * q : 4 * q + 4, :].bitcast(I32),
             )
-        for j in range(2, PACK):
-            nc.sync.dma_start(w_planes[j][:], w_rows[:, j, :])
-
-        x_rows = xT[0].rearrange("(p j) r -> p j r", j=PACK)
-        x_first = tile([P, PACK, K_PASS], F32, "x_first")
-        nc.sync.dma_start(x_first[:], x_rows[:, :, 0:K_PASS])
-        v_word_table = tile([P, T], U32, "v_word_table")
-        nc.sync.dma_start(v_word_table[:].bitcast(I32), v_words[0].rearrange("p c j -> p (c j)").bitcast(I32))
-        x_second = [tile([P, PACK, K_PASS // 2], F32, "x_second%d" % h) for h in range(2)]
-        for h in range(2):
-            r0 = K_PASS + h * (K_PASS // 2)
-            nc.sync.dma_start(x_second[h][:], x_rows[:, :, r0 : r0 + K_PASS // 2])
-        m_raw = [tile([P, PACK, D], F32, "m_raw%d" % g) for g in range(ROW_PASSES)]
-        m_rows = xm[0].rearrange("(g p t) d -> g p t d", p=P, t=PACK)
-        for g in range(ROW_PASSES):
-            nc.sync.dma_start(m_raw[g][:], m_rows[g])
-
-        windows = [tile([P, T], F32, "window%d" % k) for k in range(D_TILES)]
-        for k in range(D_TILES):
-            (nc.vector if k < 2 else nc.gpsimd).memset(windows[k][:].bitcast(I32), 0)
-
-        neg_weight = tile([P, ROW_PASSES, PACK], F32, "neg_weight")
-        upper = tile([P, ROW_PASSES, PACK], F32, "upper")
-        lower = tile([P, ROW_PASSES, PACK], F32, "lower")
-        nc.scalar.activation(neg_weight[:], weight[:], COPY, scale=-1.0)
-        nc.vector.tensor_tensor(upper[:], weight[:], neg_weight[:], ALU.max)
-        nc.vector.tensor_tensor(lower[:], weight[:], neg_weight[:], ALU.min)
+        nc.sync.dma_start(w_planes[PACK - 1][:], w_rows[:, PACK - 1, :])
 
         w_picked = tile([P, PACK, N], F32, "w_picked")
         v_scale = tile([P, N], U8, "v_scale")
@@ -95,6 +92,16 @@ def tile_attend_gds_hub_kernel(tc, xT, wT, v_words, v_scales, wt, xm, offs, out)
             nc.vector.tensor_copy(w_picked[:, j, :], w_planes[j][:].indirect(offsets[:]))
             if j == PACK - 2:
                 nc.vector.tensor_copy(v_scale[:], v_scale_table[:].indirect(offsets[:]))
+
+        x_rows = xT[0].rearrange("(p j) r -> p j r", j=PACK)
+        x_first = tile([P, PACK, K_PASS], F32, "x_first", "w_plane0")
+        nc.sync.dma_start(x_first[:], x_rows[:, :, 0:K_PASS])
+        v_word_table = tile([P, T], U32, "v_word_table", "w_plane1")
+        nc.sync.dma_start(v_word_table[:].bitcast(I32), v_words[0].rearrange("p c j -> p (c j)").bitcast(I32))
+        x_second = [tile([P, PACK, K_PASS // 2], F32, "x_second%d" % h, ("w_plane2", "v_scale_table")[h]) for h in range(2)]
+        for h in range(2):
+            r0 = K_PASS + h * (K_PASS // 2)
+            nc.sync.dma_start(x_second[h][:], x_rows[:, :, r0 : r0 + K_PASS // 2])
 
         w_neg = tile([P, N, PACK], BF16, "w_neg")
         s = W_SLOTS_ON_SCALAR
@@ -104,47 +111,95 @@ def tile_attend_gds_hub_kernel(tc, xT, wT, v_words, v_scales, wt, xm, offs, out)
         w_scale = tile([P, N], U8, "w_scale")
         nc.vector.quantize_mx(w_codes[:].bitcast(E4M3), w_scale[:], w_neg[:].rearrange("p c t -> p (c t)"))
 
-        x_codes = [tile([P, K_PASS], U32, "x_codes%d" % g) for g in range(ROW_PASSES)]
-        x_scale = [tile([P, K_PASS], U8, "x_scale%d" % g) for g in range(ROW_PASSES)]
+        x_codes = {}
+        x_scale = {}
 
-        def by_row(ap):
-            return ap.rearrange("p j (m t) -> p m j t", t=PACK)
+        def quantize_x(g, t, x_dealt, reuses=None):
+            x_codes[g, t] = tile([P, 2 * P], U32, "x_codes%d_%d" % (g, t), reuses)
+            x_scale[g, t] = tile([P, 2 * P], U8, "x_scale%d_%d" % (g, t))
+            source = x_dealt[:, t : t + 2].rearrange("p t m j -> p (t m j)")
+            nc.vector.quantize_mx(x_codes[g, t][:].bitcast(E4M3), x_scale[g, t][:], source)
 
         def score_pass(bank, g, t, codes, scale, first):
-            cols = slice(t * P, (t + 1) * P)
+            pair = (g, t - t % 2)
+            cols = slice(t % 2 * P, (t % 2 + 1) * P)
             nc.tensor.matmul_mx(
                 bank[:],
-                lhsT=x_codes[g][:, cols].bitcast(E4M3),
-                lhsT_scale=x_scale[g][:, cols],
+                lhsT=x_codes[pair][:, cols].bitcast(E4M3),
+                lhsT_scale=x_scale[pair][:, cols],
                 rhs=codes[:].bitcast(E4M3),
                 rhs_scale=scale[:],
                 start=first,
                 stop=not first,
             )
 
-        g_planes = []
         g_codes = [tile([P, N], U32, "g_codes%d" % g) for g in range(ROW_PASSES)]
         g_scale = [tile([P, N], U8, "g_scale%d" % g) for g in range(ROW_PASSES)]
 
-        def weigh_and_clip(bank, g, t):
-            weighted = tile([P, N], F32, "weighted%d_%d" % (g, t))
-            nc.scalar.activation(weighted[:], bank[:], COPY, scale=neg_weight[:, g, t : t + 1])
+        def weigh_and_clip(bank, g, t, weighted, g_planes):
+            nc.scalar.activation(weighted[:, t, :], bank[:], COPY, scale=neg_weight[:, g, t : t + 1])
             nc.vector.tensor_scalar(
-                g_planes[g][:, t, :], weighted[:], lower[:, g, t : t + 1], upper[:, g, t : t + 1], ALU.max, ALU.min
+                g_planes[:, t, :], weighted[:, t, :], lower[:, g, t : t + 1], upper[:, g, t : t + 1], ALU.max, ALU.min
             )
 
         def quantize_g(g, slots, source):
             nc.vector.quantize_mx(
-                g_codes[g][:, slots].bitcast(E5M2), g_scale[g][:, slots], source[:].rearrange("p c t -> p (c t)")
+                g_codes[g][:, slots].bitcast(E5M2), g_scale[g][:, slots], source.rearrange("p c t -> p (c t)")
             )
+
+        x_dealt = tile([P, PACK, P, PACK], BF16, "x_dealt", "weight")
+        h = X_COLUMNS_ON_SCALAR
+        nc.scalar.copy(dealt(x_dealt[:])[:, 0:h], by_row(x_first[:])[:, 0:h])
+        nc.vector.tensor_copy(dealt(x_dealt[:])[:, h:P], by_row(x_first[:])[:, h:P])
+        quantize_x(0, 0, x_dealt)
+
+        m_rows = xm[0].rearrange("(g p t) d -> g p t d", p=P, t=PACK)
+        m_raw = [tile([P, PACK, D], F32, "m_raw%d" % g, ("w_picked", "w_plane0")[g]) for g in range(ROW_PASSES)]
+        for g in range(ROW_PASSES):
+            nc.sync.dma_start(m_raw[g][:], m_rows[g])
+
+        v_codes = tile([P, N], U32, "v_codes", "w_neg")
+        nc.vector.tensor_copy(v_codes[:], v_word_table[:].indirect(offsets[:]))
+        quantize_x(0, 2, x_dealt, "w_plane1")
+
+        x_dealt = tile([P, PACK, P, PACK], BF16, "x_dealt1")
+        for h, copy in enumerate((nc.scalar.copy, nc.vector.tensor_copy)):
+            copy(dealt(x_dealt[:])[:, h * (P // 2) : (h + 1) * (P // 2)], by_row(x_second[h][:]))
+        for t in range(0, PACK, 2):
+            quantize_x(1, t, x_dealt)
+
+        weighted = tile([P, PACK, N], F32, "weighted_first", "w_plane2")
+        g_first = tile([P, PACK, N], BF16, "g_first", "x_dealt1")
+        for group in (range(0, 2), range(2, 3), range(3, 4)):
+            banks = {t: score_psum.tile([P, N], F32, name="first_bank%d" % t) for t in group}
+            for t in group:
+                score_pass(banks[t], 0, t, w_codes, w_scale, True)
+            for t in group:
+                score_pass(banks[t], 0, t, v_codes, v_scale, False)
+            for t in group:
+                weigh_and_clip(banks[t], 0, t, weighted, g_first)
+
+        s = HALF
+        g_first_low = tile([P, s, PACK], BF16, "g_first_low")
+        nc.vector.tensor_copy(woven(g_first_low[:]), planar(g_first[:, :, 0:s]))
+
+        weighted = tile([P, PACK, N], F32, "weighted_second")
+        g_second = tile([P, PACK, N], BF16, "g_second")
+        for t in range(PACK):
+            bank = score_psum.tile([P, N], F32, name=("second_bank0", "second_bank1", "first_bank0", "first_bank1")[t])
+            score_pass(bank, 1, t, w_codes, w_scale, True)
+            score_pass(bank, 1, t, v_codes, v_scale, False)
+            weigh_and_clip(bank, 1, t, weighted, g_second)
+            if t == 0:
+                quantize_g(0, slice(0, s), g_first_low[:])
 
         m_codes = [tile([P, ROW_PASSES * P], U32, "m_codes%d" % k) for k in range(D_TILES)]
         m_scale = [tile([P, ROW_PASSES * P], U8, "m_scale%d" % k) for k in range(D_TILES)]
 
-        def weave_m(k, reuses):
+        def weave_m(k, reuses, copy):
             m_woven = tile([P, ROW_PASSES, P, PACK], BF16, "m_woven%d" % k, reuses)
             for g in range(ROW_PASSES):
-                nc.scalar.copy(woven(m_woven[:, g]), planar(m_raw[g][:, :, k * P : (k + 1) * P]))
+                copy(woven(m_woven[:, g]), planar(m_raw[g][:, :, k * P : (k + 1) * P]))
             return m_woven
 
         def quantize_m(k, m_woven):
@@ -165,63 +220,27 @@ def tile_attend_gds_hub_kernel(tc, xT, wT, v_words, v_scales, wt, xm, offs, out)
                 )
             return bank
 
-        x_dealt = tile([P, PACK, P, PACK], BF16, "x_dealt0", "w_plane3")
-        dst = x_dealt[:].rearrange("p t m j -> p m j t")
-        h = X_COLUMNS_ON_SCALAR
-        nc.scalar.copy(dst[:, 0:h], by_row(x_first[:])[:, 0:h])
-        nc.vector.tensor_copy(dst[:, h:P], by_row(x_first[:])[:, h:P])
-        nc.vector.quantize_mx(x_codes[0][:].bitcast(E4M3), x_scale[0][:], x_dealt[:].rearrange("p t m j -> p (t m j)"))
-
-        v_codes = tile([P, N], U32, "v_codes", "w_plane3")
-        nc.vector.tensor_copy(v_codes[:], v_word_table[:].indirect(offsets[:]))
-
-        x_dealt = tile([P, PACK, P, PACK], BF16, "x_dealt1", "v_word_table")
-        dst = x_dealt[:].rearrange("p t m j -> p m j t")
-        for h in range(2):
-            nc.vector.tensor_copy(dst[:, h * (P // 2) : (h + 1) * (P // 2)], by_row(x_second[h][:]))
-        for t in range(PACK):
-            cols = slice(t * P, (t + 1) * P)
-            nc.vector.quantize_mx(
-                x_codes[1][:, cols].bitcast(E4M3), x_scale[1][:, cols], x_dealt[:, t].rearrange("p m j -> p (m j)")
-            )
-        g_planes.append(tile([P, PACK, N], BF16, "g_planes0", "v_word_table"))
-        g_planes.append(tile([P, PACK, N], BF16, "g_planes1"))
-        for pair in range(0, PACK, 2):
-            banks = [score_psum.tile([P, N], F32, name="first_bank%d" % i) for i in range(2)]
-            for i in range(2):
-                score_pass(banks[i], 0, pair + i, w_codes, w_scale, True)
-            for i in range(2):
-                score_pass(banks[i], 0, pair + i, v_codes, v_scale, False)
-            for i in range(2):
-                weigh_and_clip(banks[i], 0, pair + i)
-        g_first_low = tile([P, HALF, PACK], BF16, "g_first_low")
-        nc.vector.tensor_copy(woven(g_first_low[:]), planar(g_planes[0][:, :, 0:HALF]))
-
-        for t in range(PACK):
-            bank = score_psum.tile([P, N], F32, name="second_bank%d" % t)
-            score_pass(bank, 1, t, w_codes, w_scale, True)
-            score_pass(bank, 1, t, v_codes, v_scale, False)
-            weigh_and_clip(bank, 1, t)
-            if t == 0:
-                quantize_g(0, slice(0, HALF), g_first_low)
-
-        g_second = tile([P, N, PACK], BF16, "g_second")
-        nc.vector.tensor_copy(woven(g_second[:]), planar(g_planes[1][:]))
-        m_woven = weave_m(0, "x_codes1")
-        g_first_high = tile([P, HALF, PACK], BF16, "g_first_high", "neg_weight")
-        nc.scalar.copy(woven(g_first_high[:]), planar(g_planes[0][:, :, HALF:N]))
+        g_second_woven = tile([P, N, PACK], BF16, "g_second_woven")
+        nc.vector.tensor_copy(woven(g_second_woven[:]), planar(g_second[:]))
+        m_woven = weave_m(0, "x_codes1_2", nc.scalar.copy)
+        g_first_high = tile([P, N - s, PACK], BF16, "g_first_high", "neg_weight")
+        nc.scalar.copy(woven(g_first_high[:]), planar(g_first[:, :, s:N]))
         quantize_m(0, m_woven)
-        quantize_g(1, slice(0, N), g_second)
-        quantize_g(0, slice(HALF, N), g_first_high)
+        quantize_g(1, slice(0, N), g_second_woven[:])
+        quantize_g(0, slice(HALF, N), g_first_high[:])
 
-        m_woven = weave_m(1, "g_planes1")
-        quantize_m(1, m_woven)
+        quantize_m(1, weave_m(1, "upper", nc.scalar.copy))
+        m_last = weave_m(3, "g_second_woven", nc.vector.tensor_copy)
+        quantize_m(2, weave_m(2, "lower", nc.scalar.copy))
+        quantize_m(3, m_last)
         for k in range(D_TILES):
             bank = gradient_passes(k)
-            if 1 <= k < D_TILES - 1:
-                m_woven = weave_m(k + 1, "m_codes%d" % (k - 1))
-                quantize_m(k + 1, m_woven)
             grad = tile([P, N], F32, "grad%d" % k)
             nc.scalar.copy(grad[:], bank[:])
             nc.vector.tensor_copy(windows[k][:].indirect(offsets[:]), grad[:])
-            nc.sync.dma_start(out[k * P : (k + 1) * P, :], windows[k][:])
+            rows = slice(k * P, (k + 1) * P)
+            if k < D_TILES - 1:
+                nc.sync.dma_start(out[rows, :], windows[k][:])
+            else:
+                nc.sync.dma_start(out[rows, 0 : T // 2], windows[k][:, 0 : T // 2])
+                nc.scalar.dma_start(out[rows, T // 2 : T], windows[k][:, T // 2 : T])

@@ -26,7 +26,7 @@ HALF = N // 2
 
 W_SLOTS_ON_SCALAR = 224
 X_COLUMNS_ON_SCALAR = 40
-WINDOWS_ON_VECTOR = 2
+WINDOWS_ON_VECTOR = 4
 
 
 def woven(ap):
@@ -127,14 +127,17 @@ def tile_attend_gds_hub_kernel(tc, xT, wT, v_words, v_scales, wt, xm, offs, out)
                 bank[:],
                 lhsT=x_codes[pair][:, cols].bitcast(E4M3),
                 lhsT_scale=x_scale[pair][:, cols],
-                rhs=codes[:].bitcast(E4M3),
-                rhs_scale=scale[:],
+                rhs=codes.bitcast(E4M3),
+                rhs_scale=scale,
                 start=first,
                 stop=not first,
             )
 
-        g_codes = [tile([P, N], U32, "g_codes%d" % g) for g in range(ROW_PASSES)]
-        g_scale = [tile([P, N], U8, "g_scale%d" % g) for g in range(ROW_PASSES)]
+        g_codes = [tile([P, HALF + N], U32, "g_codes%d" % g) for g in range(ROW_PASSES)]
+        g_scale = [tile([P, HALF + N], U8, "g_scale%d" % g) for g in range(ROW_PASSES)]
+        for g in range(ROW_PASSES):
+            nc.gpsimd.memset(g_codes[g][:, 0:HALF].bitcast(I32), 0)
+            nc.gpsimd.memset(g_scale[g][:, 0:HALF], 0)
 
         def weigh_and_clip(bank, g, t, weighted, g_planes):
             nc.scalar.activation(weighted[:, t, :], bank[:], COPY, scale=neg_weight[:, g, t : t + 1])
@@ -142,9 +145,10 @@ def tile_attend_gds_hub_kernel(tc, xT, wT, v_words, v_scales, wt, xm, offs, out)
                 g_planes[:, t, :], weighted[:, t, :], lower[:, g, t : t + 1], upper[:, g, t : t + 1], ALU.max, ALU.min
             )
 
-        def quantize_g(g, slots, source):
+        def quantize_g(g, half, source):
+            cols = slice((half + 1) * HALF, (half + 2) * HALF)
             nc.vector.quantize_mx(
-                g_codes[g][:, slots].bitcast(E5M2), g_scale[g][:, slots], source.rearrange("p c t -> p (c t)")
+                g_codes[g][:, cols].bitcast(E5M2), g_scale[g][:, cols], source[:].rearrange("p c t -> p (c t)")
             )
 
         x_dealt = tile([P, PACK, P, PACK], BF16, "x_dealt", "weight")
@@ -154,9 +158,12 @@ def tile_attend_gds_hub_kernel(tc, xT, wT, v_words, v_scales, wt, xm, offs, out)
         quantize_x(0, 0, x_dealt)
 
         m_rows = xm[0].rearrange("(g p t) d -> g p t d", p=P, t=PACK)
-        m_raw = [tile([P, PACK, D], F32, "m_raw%d" % g, ("w_picked", "w_plane0")[g]) for g in range(ROW_PASSES)]
-        for g in range(ROW_PASSES):
-            nc.sync.dma_start(m_raw[g][:], m_rows[g])
+        m_raw = []
+        for u, reuses in enumerate(("w_picked", "w_plane0")):
+            m_half = tile([P, ROW_PASSES, PACK, D // 2], F32, "m_raw%d" % u, reuses)
+            for g in range(ROW_PASSES):
+                nc.sync.dma_start(m_half[:, g], m_rows[g][:, :, u * (D // 2) : (u + 1) * (D // 2)])
+            m_raw.append(m_half)
 
         v_codes = tile([P, N], U32, "v_codes", "w_neg")
         nc.vector.tensor_copy(v_codes[:], v_word_table[:].indirect(offsets[:]))
@@ -173,74 +180,82 @@ def tile_attend_gds_hub_kernel(tc, xT, wT, v_words, v_scales, wt, xm, offs, out)
         for group in (range(0, 2), range(2, 3), range(3, 4)):
             banks = {t: score_psum.tile([P, N], F32, name="first_bank%d" % t) for t in group}
             for t in group:
-                score_pass(banks[t], 0, t, w_codes, w_scale, True)
+                score_pass(banks[t], 0, t, w_codes[:], w_scale[:], True)
             for t in group:
-                score_pass(banks[t], 0, t, v_codes, v_scale, False)
+                score_pass(banks[t], 0, t, v_codes[:], v_scale[:], False)
             for t in group:
                 weigh_and_clip(banks[t], 0, t, weighted, g_first)
 
-        s = HALF
-        g_first_low = tile([P, s, PACK], BF16, "g_first_low")
-        nc.vector.tensor_copy(woven(g_first_low[:]), planar(g_first[:, :, 0:s]))
+        def weave_g(name, planes, copy, reuses=None):
+            g_woven = tile([P, HALF, PACK], BF16, name, reuses)
+            copy(woven(g_woven[:]), planar(planes))
+            return g_woven
 
-        weighted = tile([P, PACK, N], F32, "weighted_second")
-        g_second = tile([P, PACK, N], BF16, "g_second")
-        for t in range(PACK):
-            bank = score_psum.tile([P, N], F32, name=("second_bank0", "second_bank1", "first_bank0", "first_bank1")[t])
-            score_pass(bank, 1, t, w_codes, w_scale, True)
-            score_pass(bank, 1, t, v_codes, v_scale, False)
-            weigh_and_clip(bank, 1, t, weighted, g_second)
-            if t == 0:
-                quantize_g(0, slice(0, s), g_first_low[:])
+        def second_pass(half, bank_names):
+            slots = slice(half * HALF, (half + 1) * HALF)
+            weighted = tile([P, PACK, HALF], F32, "weighted_second%d" % half)
+            g_second = tile([P, PACK, HALF], BF16, "g_second%d" % half)
+            for t in range(PACK):
+                bank = score_psum.tile([P, HALF], F32, name=bank_names[t])
+                score_pass(bank, 1, t, w_codes[:, slots], w_scale[:, slots], True)
+                score_pass(bank, 1, t, v_codes[:, slots], v_scale[:, slots], False)
+                weigh_and_clip(bank, 1, t, weighted, g_second)
+            return g_second
 
         m_codes = [tile([P, ROW_PASSES * P], U32, "m_codes%d" % k) for k in range(D_TILES)]
         m_scale = [tile([P, ROW_PASSES * P], U8, "m_scale%d" % k) for k in range(D_TILES)]
 
-        def weave_m(k, reuses, copy):
+        def weave_m(k, reuses=None):
             m_woven = tile([P, ROW_PASSES, P, PACK], BF16, "m_woven%d" % k, reuses)
             for g in range(ROW_PASSES):
-                copy(woven(m_woven[:, g]), planar(m_raw[g][:, :, k * P : (k + 1) * P]))
+                nc.scalar.copy(woven(m_woven[:, g]), planar(m_raw[k // 2][:, g, :, k % 2 * P : (k % 2 + 1) * P]))
             return m_woven
 
         def quantize_m(k, m_woven):
             nc.vector.quantize_mx(m_codes[k][:].bitcast(E4M3), m_scale[k][:], m_woven[:].rearrange("p g c t -> p (g c t)"))
 
-        def gradient_passes(k):
+        def gradient_passes(k, first_column, order):
             bank = grad_psum.tile([P, N], F32, name="grad_bank")
-            for g in reversed(range(ROW_PASSES)):
+            moving = slice(first_column, first_column + N)
+            for g in order:
                 cols = slice(g * P, (g + 1) * P)
                 nc.tensor.matmul_mx(
                     bank[:],
                     lhsT=m_codes[k][:, cols].bitcast(E4M3),
                     lhsT_scale=m_scale[k][:, cols],
-                    rhs=g_codes[g][:].bitcast(E5M2),
-                    rhs_scale=g_scale[g][:],
-                    start=(g == ROW_PASSES - 1),
-                    stop=(g == 0),
+                    rhs=g_codes[g][:, moving].bitcast(E5M2),
+                    rhs_scale=g_scale[g][:, moving],
+                    start=(g == order[0]),
+                    stop=(g == order[-1]),
                 )
             return bank
 
-        g_second_woven = tile([P, N, PACK], BF16, "g_second_woven")
-        nc.vector.tensor_copy(woven(g_second_woven[:]), planar(g_second[:]))
-        m_woven = weave_m(0, "x_codes1_2", nc.scalar.copy)
-        g_first_high = tile([P, N - s, PACK], BF16, "g_first_high", "neg_weight")
-        nc.scalar.copy(woven(g_first_high[:]), planar(g_first[:, :, s:N]))
-        quantize_m(0, m_woven)
-        quantize_g(1, slice(0, N), g_second_woven[:])
-        quantize_g(0, slice(HALF, N), g_first_high[:])
+        first_low = weave_g("first_low", g_first[:, :, 0:HALF], nc.vector.tensor_copy)
+        g_second = second_pass(0, ("second_bank0", "second_bank1", "first_bank0", "first_bank1"))
+        quantize_g(0, 0, first_low)
+        second_low = weave_g("second_low", g_second[:], nc.vector.tensor_copy)
+        quantize_m(0, weave_m(0, "w_plane2"))
+        quantize_g(1, 0, second_low)
 
-        quantize_m(1, weave_m(1, "upper", nc.scalar.copy))
-        m_last = weave_m(3, "g_second_woven", nc.vector.tensor_copy)
-        quantize_m(2, weave_m(2, "lower", nc.scalar.copy))
-        quantize_m(3, m_last)
+        low_bank = gradient_passes(0, 0, (0, 1))
+
+        g_second = second_pass(1, ("first_bank2", "first_bank3", "second_bank0", "second_bank1"))
+        first_high = weave_g("first_high", g_first[:, :, HALF:N], nc.scalar.copy, "neg_weight")
+        second_high = weave_g("second_high", g_second[:], nc.vector.tensor_copy)
+
+        quantize_g(0, 1, first_high)
+        quantize_g(1, 1, second_high)
+
+        grad_low = tile([P, HALF], F32, "grad_low", "g_second1")
+        nc.scalar.copy(grad_low[:], low_bank[:, HALF:N])
+        nc.vector.tensor_copy(windows[0][:].indirect(offsets[:, 0 : HALF // 16]), grad_low[:])
+
         for k in range(D_TILES):
-            bank = gradient_passes(k)
-            grad = tile([P, N], F32, "grad%d" % k)
-            nc.scalar.copy(grad[:], bank[:])
-            nc.vector.tensor_copy(windows[k][:].indirect(offsets[:]), grad[:])
-            rows = slice(k * P, (k + 1) * P)
-            if k < D_TILES - 1:
-                nc.sync.dma_start(out[rows, :], windows[k][:])
-            else:
-                nc.sync.dma_start(out[rows, 0 : T // 2], windows[k][:, 0 : T // 2])
-                nc.scalar.dma_start(out[rows, T // 2 : T], windows[k][:, T // 2 : T])
+            bank = gradient_passes(k, HALF, (0, 1))
+            if k + 1 < D_TILES:
+                quantize_m(k + 1, weave_m(k + 1, ("upper", "m_codes0", "m_codes1")[k]))
+            first_slot = HALF if k == 0 else 0
+            grad = tile([P, N - first_slot], F32, "grad%d" % k)
+            nc.scalar.copy(grad[:], bank[:, first_slot:N])
+            nc.vector.tensor_copy(windows[k][:].indirect(offsets[:, first_slot // 16 : N // 16]), grad[:])
+            nc.sync.dma_start(out[k * P : (k + 1) * P, :], windows[k][:])

@@ -23,10 +23,11 @@ K_PASS = P * PACK
 ROW_PASSES = R // K_PASS
 D_TILES = D // P
 HALF = N // 2
+QUADRANTS = 4
+PER_COLUMN = 16
 
 W_SLOTS_ON_SCALAR = 224
 X_COLUMNS_ON_SCALAR = 40
-WINDOWS_ON_VECTOR = 4
 
 
 def woven(ap):
@@ -55,7 +56,7 @@ def tile_attend_gds_hub_kernel(tc, xT, wT, v_words, v_scales, wt, xm, offs, out)
         def tile(shape, dtype, name, reuses=None):
             return keep.tile(shape, dtype, name=name, tag=reuses or name, align_bytes=64)
 
-        offsets = tile([P, N // 16], U16, "offsets")
+        offsets = tile([P, N // PER_COLUMN], U16, "offsets")
 
         weight = tile([P, ROW_PASSES, PACK], F32, "weight")
         nc.scalar.dma_start(weight[:], wt[0].rearrange("(g p t) o -> p g (t o)", p=P, t=PACK))
@@ -69,17 +70,17 @@ def tile_attend_gds_hub_kernel(tc, xT, wT, v_words, v_scales, wt, xm, offs, out)
         v_scale_table = tile([P, T], U8, "v_scale_table")
         nc.gpsimd.memset(v_scale_table[:].bitcast(I32), 0)
         windows = [tile([P, T], F32, "window%d" % k) for k in range(D_TILES)]
-        for k in range(D_TILES):
-            (nc.vector if k < WINDOWS_ON_VECTOR else nc.gpsimd).memset(windows[k][:].bitcast(I32), 0)
+        for window in windows:
+            nc.vector.memset(window[:].bitcast(I32), 0)
 
         w_planes = [tile([P, T], F32, "w_plane%d" % j) for j in range(PACK - 1)]
         w_planes.append(tile([P, T], F32, "w_plane3", "weight"))
         w_rows = wT.rearrange("(p j) c -> p j c", j=PACK)
-        for j in range(PACK - 1):
+        nc.sync.dma_start(w_planes[0][:], w_rows[:, 0, :])
+        nc.sync.dma_start(offsets[:], offs)
+        for j in range(1, PACK - 1):
             nc.sync.dma_start(w_planes[j][:], w_rows[:, j, :])
-            if j == 0:
-                nc.sync.dma_start(offsets[:], offs)
-        for q in range(4):
+        for q in range(QUADRANTS):
             nc.sync.dma_start(
                 v_scale_table[32 * q : 32 * q + 4, :].bitcast(I32),
                 v_scales[0, 4 * q : 4 * q + 4, :].bitcast(I32),
@@ -88,25 +89,29 @@ def tile_attend_gds_hub_kernel(tc, xT, wT, v_words, v_scales, wt, xm, offs, out)
 
         w_picked = tile([P, PACK, N], F32, "w_picked")
         v_scale = tile([P, N], U8, "v_scale")
-        for j in range(PACK):
+        for j in range(PACK - 1):
             nc.vector.tensor_copy(w_picked[:, j, :], w_planes[j][:].indirect(offsets[:]))
-            if j == PACK - 2:
-                nc.vector.tensor_copy(v_scale[:], v_scale_table[:].indirect(offsets[:]))
+        nc.vector.tensor_copy(v_scale[:], v_scale_table[:].indirect(offsets[:]))
+        nc.vector.tensor_copy(w_picked[:, PACK - 1, :], w_planes[PACK - 1][:].indirect(offsets[:]))
 
         x_rows = xT[0].rearrange("(p j) r -> p j r", j=PACK)
         x_first = tile([P, PACK, K_PASS], F32, "x_first", "w_plane0")
         nc.sync.dma_start(x_first[:], x_rows[:, :, 0:K_PASS])
         v_word_table = tile([P, T], U32, "v_word_table", "w_plane1")
         nc.sync.dma_start(v_word_table[:].bitcast(I32), v_words[0].rearrange("p c j -> p (c j)").bitcast(I32))
-        x_second = [tile([P, PACK, K_PASS // 2], F32, "x_second%d" % h, ("w_plane2", "v_scale_table")[h]) for h in range(2)]
-        for h in range(2):
-            r0 = K_PASS + h * (K_PASS // 2)
-            nc.sync.dma_start(x_second[h][:], x_rows[:, :, r0 : r0 + K_PASS // 2])
+        half_rows = K_PASS // 2
+        x_second = [
+            tile([P, PACK, half_rows], F32, "x_second%d" % u, reuses)
+            for u, reuses in enumerate(("w_plane2", "v_scale_table"))
+        ]
+        for u, x_half in enumerate(x_second):
+            first_row = K_PASS + u * half_rows
+            nc.sync.dma_start(x_half[:], x_rows[:, :, first_row : first_row + half_rows])
 
         w_neg = tile([P, N, PACK], BF16, "w_neg")
-        s = W_SLOTS_ON_SCALAR
-        nc.scalar.activation(woven(w_neg[:, 0:s, :]), planar(w_picked[:, :, 0:s]), COPY, scale=-1.0)
-        nc.vector.tensor_scalar(woven(w_neg[:, s:N, :]), planar(w_picked[:, :, s:N]), -1.0, None, ALU.mult)
+        w_cut = W_SLOTS_ON_SCALAR
+        nc.scalar.activation(woven(w_neg[:, 0:w_cut, :]), planar(w_picked[:, :, 0:w_cut]), COPY, scale=-1.0)
+        nc.vector.tensor_scalar(woven(w_neg[:, w_cut:N, :]), planar(w_picked[:, :, w_cut:N]), -1.0, None, ALU.mult)
         w_codes = tile([P, N], U32, "w_codes")
         w_scale = tile([P, N], U8, "w_scale")
         nc.vector.quantize_mx(w_codes[:].bitcast(E4M3), w_scale[:], w_neg[:].rearrange("p c t -> p (c t)"))
@@ -145,46 +150,47 @@ def tile_attend_gds_hub_kernel(tc, xT, wT, v_words, v_scales, wt, xm, offs, out)
                 g_planes[:, t, :], weighted[:, t, :], lower[:, g, t : t + 1], upper[:, g, t : t + 1], ALU.max, ALU.min
             )
 
-        def quantize_g(g, half, source):
+        def quantize_g(g, half, g_woven):
             cols = slice((half + 1) * HALF, (half + 2) * HALF)
             nc.vector.quantize_mx(
-                g_codes[g][:, cols].bitcast(E5M2), g_scale[g][:, cols], source[:].rearrange("p c t -> p (c t)")
+                g_codes[g][:, cols].bitcast(E5M2), g_scale[g][:, cols], g_woven[:].rearrange("p c t -> p (c t)")
             )
 
-        x_dealt = tile([P, PACK, P, PACK], BF16, "x_dealt", "weight")
-        h = X_COLUMNS_ON_SCALAR
-        nc.scalar.copy(dealt(x_dealt[:])[:, 0:h], by_row(x_first[:])[:, 0:h])
-        nc.vector.tensor_copy(dealt(x_dealt[:])[:, h:P], by_row(x_first[:])[:, h:P])
-        quantize_x(0, 0, x_dealt)
+        first_dealt = tile([P, PACK, P, PACK], BF16, "x_dealt", "weight")
+        x_cut = X_COLUMNS_ON_SCALAR
+        nc.scalar.copy(dealt(first_dealt[:])[:, 0:x_cut], by_row(x_first[:])[:, 0:x_cut])
+        nc.vector.tensor_copy(dealt(first_dealt[:])[:, x_cut:P], by_row(x_first[:])[:, x_cut:P])
+        quantize_x(0, 0, first_dealt)
 
         m_rows = xm[0].rearrange("(g p t) d -> g p t d", p=P, t=PACK)
+        half_d = D // 2
         m_raw = []
         for u, reuses in enumerate(("w_picked", "w_plane0")):
-            m_half = tile([P, ROW_PASSES, PACK, D // 2], F32, "m_raw%d" % u, reuses)
+            m_half = tile([P, ROW_PASSES, PACK, half_d], F32, "m_raw%d" % u, reuses)
             for g in range(ROW_PASSES):
-                nc.sync.dma_start(m_half[:, g], m_rows[g][:, :, u * (D // 2) : (u + 1) * (D // 2)])
+                nc.sync.dma_start(m_half[:, g], m_rows[g][:, :, u * half_d : (u + 1) * half_d])
             m_raw.append(m_half)
 
         v_codes = tile([P, N], U32, "v_codes", "w_neg")
         nc.vector.tensor_copy(v_codes[:], v_word_table[:].indirect(offsets[:]))
-        quantize_x(0, 2, x_dealt, "w_plane1")
+        quantize_x(0, 2, first_dealt, "w_plane1")
 
-        x_dealt = tile([P, PACK, P, PACK], BF16, "x_dealt1")
-        for h, copy in enumerate((nc.scalar.copy, nc.vector.tensor_copy)):
-            copy(dealt(x_dealt[:])[:, h * (P // 2) : (h + 1) * (P // 2)], by_row(x_second[h][:]))
+        second_dealt = tile([P, PACK, P, PACK], BF16, "x_dealt1")
+        for u, copy in enumerate((nc.scalar.copy, nc.vector.tensor_copy)):
+            copy(dealt(second_dealt[:])[:, u * (P // 2) : (u + 1) * (P // 2)], by_row(x_second[u][:]))
         for t in range(0, PACK, 2):
-            quantize_x(1, t, x_dealt)
+            quantize_x(1, t, second_dealt)
 
-        weighted = tile([P, PACK, N], F32, "weighted_first", "w_plane2")
+        weighted_first = tile([P, PACK, N], F32, "weighted_first", "w_plane2")
         g_first = tile([P, PACK, N], BF16, "g_first", "x_dealt1")
-        for group in (range(0, 2), range(2, 3), range(3, 4)):
+        for group in ((0, 1), (2,), (3,)):
             banks = {t: score_psum.tile([P, N], F32, name="first_bank%d" % t) for t in group}
             for t in group:
                 score_pass(banks[t], 0, t, w_codes[:], w_scale[:], True)
             for t in group:
                 score_pass(banks[t], 0, t, v_codes[:], v_scale[:], False)
             for t in group:
-                weigh_and_clip(banks[t], 0, t, weighted, g_first)
+                weigh_and_clip(banks[t], 0, t, weighted_first, g_first)
 
         def weave_g(name, planes, copy, reuses=None):
             g_woven = tile([P, HALF, PACK], BF16, name, reuses)
@@ -194,30 +200,28 @@ def tile_attend_gds_hub_kernel(tc, xT, wT, v_words, v_scales, wt, xm, offs, out)
         def second_pass(half, bank_names):
             slots = slice(half * HALF, (half + 1) * HALF)
             weighted = tile([P, PACK, HALF], F32, "weighted_second%d" % half)
-            g_second = tile([P, PACK, HALF], BF16, "g_second%d" % half)
+            g_planes = tile([P, PACK, HALF], BF16, "g_second%d" % half)
             for t in range(PACK):
                 bank = score_psum.tile([P, HALF], F32, name=bank_names[t])
                 score_pass(bank, 1, t, w_codes[:, slots], w_scale[:, slots], True)
                 score_pass(bank, 1, t, v_codes[:, slots], v_scale[:, slots], False)
-                weigh_and_clip(bank, 1, t, weighted, g_second)
-            return g_second
+                weigh_and_clip(bank, 1, t, weighted, g_planes)
+            return g_planes
 
         m_codes = [tile([P, ROW_PASSES * P], U32, "m_codes%d" % k) for k in range(D_TILES)]
         m_scale = [tile([P, ROW_PASSES * P], U8, "m_scale%d" % k) for k in range(D_TILES)]
 
-        def weave_m(k, reuses=None):
+        def quantize_m(k, reuses):
             m_woven = tile([P, ROW_PASSES, P, PACK], BF16, "m_woven%d" % k, reuses)
             for g in range(ROW_PASSES):
                 nc.scalar.copy(woven(m_woven[:, g]), planar(m_raw[k // 2][:, g, :, k % 2 * P : (k % 2 + 1) * P]))
-            return m_woven
+            source = m_woven[:].rearrange("p g c t -> p (g c t)")
+            nc.vector.quantize_mx(m_codes[k][:].bitcast(E4M3), m_scale[k][:], source)
 
-        def quantize_m(k, m_woven):
-            nc.vector.quantize_mx(m_codes[k][:].bitcast(E4M3), m_scale[k][:], m_woven[:].rearrange("p g c t -> p (g c t)"))
-
-        def gradient_passes(k, first_column, order):
+        def gradient_passes(k, first_column):
             bank = grad_psum.tile([P, N], F32, name="grad_bank")
             moving = slice(first_column, first_column + N)
-            for g in order:
+            for g in range(ROW_PASSES):
                 cols = slice(g * P, (g + 1) * P)
                 nc.tensor.matmul_mx(
                     bank[:],
@@ -225,37 +229,36 @@ def tile_attend_gds_hub_kernel(tc, xT, wT, v_words, v_scales, wt, xm, offs, out)
                     lhsT_scale=m_scale[k][:, cols],
                     rhs=g_codes[g][:, moving].bitcast(E5M2),
                     rhs_scale=g_scale[g][:, moving],
-                    start=(g == order[0]),
-                    stop=(g == order[-1]),
+                    start=(g == 0),
+                    stop=(g == ROW_PASSES - 1),
                 )
             return bank
 
         first_low = weave_g("first_low", g_first[:, :, 0:HALF], nc.vector.tensor_copy)
-        g_second = second_pass(0, ("second_bank0", "second_bank1", "first_bank0", "first_bank1"))
+        second_low_planes = second_pass(0, ("second_bank0", "second_bank1", "first_bank0", "first_bank1"))
         quantize_g(0, 0, first_low)
-        second_low = weave_g("second_low", g_second[:], nc.vector.tensor_copy)
-        quantize_m(0, weave_m(0, "w_plane2"))
+        second_low = weave_g("second_low", second_low_planes[:], nc.vector.tensor_copy)
+        quantize_m(0, "w_plane2")
         quantize_g(1, 0, second_low)
+        low_bank = gradient_passes(0, 0)
 
-        low_bank = gradient_passes(0, 0, (0, 1))
-
-        g_second = second_pass(1, ("first_bank2", "first_bank3", "second_bank0", "second_bank1"))
+        second_high_planes = second_pass(1, ("first_bank2", "first_bank3", "second_bank0", "second_bank1"))
         first_high = weave_g("first_high", g_first[:, :, HALF:N], nc.scalar.copy, "neg_weight")
-        second_high = weave_g("second_high", g_second[:], nc.vector.tensor_copy)
-
+        second_high = weave_g("second_high", second_high_planes[:], nc.vector.tensor_copy)
         quantize_g(0, 1, first_high)
         quantize_g(1, 1, second_high)
 
-        grad_low = tile([P, HALF], F32, "grad_low", "g_second1")
+        grad_low = tile([P, HALF], F32, "grad_low", "weighted_second1")
         nc.scalar.copy(grad_low[:], low_bank[:, HALF:N])
-        nc.vector.tensor_copy(windows[0][:].indirect(offsets[:, 0 : HALF // 16]), grad_low[:])
+        nc.vector.tensor_copy(windows[0][:].indirect(offsets[:, 0 : HALF // PER_COLUMN]), grad_low[:])
 
         for k in range(D_TILES):
-            bank = gradient_passes(k, HALF, (0, 1))
+            bank = gradient_passes(k, HALF)
             if k + 1 < D_TILES:
-                quantize_m(k + 1, weave_m(k + 1, ("upper", "m_codes0", "m_codes1")[k]))
+                quantize_m(k + 1, "upper" if k == 0 else "m_codes%d" % (k - 1))
             first_slot = HALF if k == 0 else 0
             grad = tile([P, N - first_slot], F32, "grad%d" % k)
             nc.scalar.copy(grad[:], bank[:, first_slot:N])
-            nc.vector.tensor_copy(windows[k][:].indirect(offsets[:, first_slot // 16 : N // 16]), grad[:])
+            slots_left = offsets[:, first_slot // PER_COLUMN : N // PER_COLUMN]
+            nc.vector.tensor_copy(windows[k][:].indirect(slots_left), grad[:])
             nc.sync.dma_start(out[k * P : (k + 1) * P, :], windows[k][:])

from contextlib import ExitStack

import concourse.mybir as mybir

N, T, D, R = 512, 2048, 512, 1024
FLOPS = 3 * 2 * N * D * R

F32 = mybir.dt.float32
BF16 = mybir.dt.bfloat16
I32 = mybir.dt.int32
U32 = mybir.dt.uint32
U16 = mybir.dt.uint16
U8 = mybir.dt.uint8
E4M3 = mybir.dt.float8_e4m3fn_x4
E5M2 = mybir.dt.float8_e5m2_x4
ALU = mybir.AluOpType
COPY = mybir.ActivationFunctionType.Copy
ABS = mybir.ActivationFunctionType.Abs

P = 128
PACK = 4
K_PASS = P * PACK
ROW_PASSES = R // K_PASS
D_TILES = D // P
HALF = N // 2
QUADRANTS = 4
PER_COLUMN = 16

W_SLOTS_ON_SCALAR = 224
X_COLUMNS_ON_SCALAR = 40


def woven(ap):
    return ap.rearrange("p (c i) t -> p c t i", i=4)


def planar(ap):
    return ap.rearrange("p t (c i) -> p c t i", i=4)


def by_row(ap):
    return ap.rearrange("p j (m t) -> p m j t", t=PACK)


def dealt(ap):
    return ap.rearrange("p t m j -> p m j t")


def tile_attend_gds_hub_kernel(tc, xT, wT, v_words, v_scales, wt, xm, offs, out):
    nc = tc.nc
    with ExitStack() as ctx:
        keep = ctx.enter_context(tc.tile_pool(name="keep", bufs=1))
        score_psum = ctx.enter_context(tc.psum_pool(name="score_psum", bufs=1))
        grad_psum = ctx.enter_context(tc.psum_pool(name="grad_psum", bufs=2))

        def tile(shape, dtype, name, reuses=None):
            return keep.tile(shape, dtype, name=name, tag=reuses or name, align_bytes=64)

        offsets = tile([P, N // PER_COLUMN], U16, "offsets")

        weight = tile([P, ROW_PASSES, PACK], F32, "weight")
        nc.scalar.dma_start(weight[:], wt[0].rearrange("(g p t) o -> p g (t o)", p=P, t=PACK))
        neg_weight = tile([P, ROW_PASSES, PACK], F32, "neg_weight")
        upper = tile([P, ROW_PASSES, PACK], F32, "upper")
        lower = tile([P, ROW_PASSES, PACK], F32, "lower")
        nc.scalar.activation(neg_weight[:], weight[:], COPY, scale=-1.0)
        nc.scalar.activation(upper[:], weight[:], ABS)
        nc.scalar.activation(lower[:], upper[:], COPY, scale=-1.0)

        v_scale_table = tile([P, T], U8, "v_scale_table")
        nc.gpsimd.memset(v_scale_table[:].bitcast(I32), 0)
        windows = [tile([P, T], F32, "window%d" % k) for k in range(D_TILES)]
        for window in windows:
            nc.vector.memset(window[:].bitcast(I32), 0)

        w_planes = [tile([P, T], F32, "w_plane%d" % j) for j in range(PACK - 1)]
        w_planes.append(tile([P, T], F32, "w_plane3", "weight"))
        w_rows = wT.rearrange("(p j) c -> p j c", j=PACK)
        nc.sync.dma_start(w_planes[0][:], w_rows[:, 0, :])
        nc.sync.dma_start(offsets[:], offs)
        for j in range(1, PACK - 1):
            nc.sync.dma_start(w_planes[j][:], w_rows[:, j, :])
        for q in range(QUADRANTS):
            nc.sync.dma_start(
                v_scale_table[32 * q : 32 * q + 4, :].bitcast(I32),
                v_scales[0, 4 * q : 4 * q + 4, :].bitcast(I32),
            )
        nc.sync.dma_start(w_planes[PACK - 1][:], w_rows[:, PACK - 1, :])

        w_picked = tile([P, PACK, N], F32, "w_picked")
        v_scale = tile([P, N], U8, "v_scale")
        for j in range(PACK - 1):
            nc.vector.tensor_copy(w_picked[:, j, :], w_planes[j][:].indirect(offsets[:]))
        nc.vector.tensor_copy(v_scale[:], v_scale_table[:].indirect(offsets[:]))
        nc.vector.tensor_copy(w_picked[:, PACK - 1, :], w_planes[PACK - 1][:].indirect(offsets[:]))

        x_rows = xT[0].rearrange("(p j) r -> p j r", j=PACK)
        x_first = tile([P, PACK, K_PASS], F32, "x_first", "w_plane0")
        nc.sync.dma_start(x_first[:], x_rows[:, :, 0:K_PASS])
        v_word_table = tile([P, T], U32, "v_word_table", "w_plane1")
        nc.sync.dma_start(v_word_table[:].bitcast(I32), v_words[0].rearrange("p c j -> p (c j)").bitcast(I32))
        half_rows = K_PASS // 2
        x_second = [
            tile([P, PACK, half_rows], F32, "x_second%d" % u, reuses)
            for u, reuses in enumerate(("w_plane2", "v_scale_table"))
        ]
        for u, x_half in enumerate(x_second):
            first_row = K_PASS + u * half_rows
            nc.sync.dma_start(x_half[:], x_rows[:, :, first_row : first_row + half_rows])

        w_neg = tile([P, N, PACK], BF16, "w_neg")
        w_cut = W_SLOTS_ON_SCALAR
        nc.scalar.activation(woven(w_neg[:, 0:w_cut, :]), planar(w_picked[:, :, 0:w_cut]), COPY, scale=-1.0)
        nc.vector.tensor_scalar(woven(w_neg[:, w_cut:N, :]), planar(w_picked[:, :, w_cut:N]), -1.0, None, ALU.mult)
        w_codes = tile([P, N], U32, "w_codes")
        w_scale = tile([P, N], U8, "w_scale")
        nc.vector.quantize_mx(w_codes[:].bitcast(E4M3), w_scale[:], w_neg[:].rearrange("p c t -> p (c t)"))

        x_codes = {}
        x_scale = {}

        def quantize_x(g, t, x_dealt, reuses=None):
            x_codes[g, t] = tile([P, 2 * P], U32, "x_codes%d_%d" % (g, t), reuses)
            x_scale[g, t] = tile([P, 2 * P], U8, "x_scale%d_%d" % (g, t))
            source = x_dealt[:, t : t + 2].rearrange("p t m j -> p (t m j)")
            nc.vector.quantize_mx(x_codes[g, t][:].bitcast(E4M3), x_scale[g, t][:], source)

        def score_pass(bank, g, t, codes, scale, first):
            pair = (g, t - t % 2)
            cols = slice(t % 2 * P, (t % 2 + 1) * P)
            nc.tensor.matmul_mx(
                bank[:],
                lhsT=x_codes[pair][:, cols].bitcast(E4M3),
                lhsT_scale=x_scale[pair][:, cols],
                rhs=codes.bitcast(E4M3),
                rhs_scale=scale,
                start=first,
                stop=not first,
            )

        g_codes = [tile([P, HALF + N], U32, "g_codes%d" % g) for g in range(ROW_PASSES)]
        g_scale = [tile([P, HALF + N], U8, "g_scale%d" % g) for g in range(ROW_PASSES)]
        for g in range(ROW_PASSES):
            nc.gpsimd.memset(g_codes[g][:, 0:HALF].bitcast(I32), 0)
            nc.gpsimd.memset(g_scale[g][:, 0:HALF], 0)

        def weigh_and_clip(bank, g, t, weighted, g_planes):
            nc.scalar.activation(weighted[:, t, :], bank[:], COPY, scale=neg_weight[:, g, t : t + 1])
            nc.vector.tensor_scalar(
                g_planes[:, t, :], weighted[:, t, :], lower[:, g, t : t + 1], upper[:, g, t : t + 1], ALU.max, ALU.min
            )

        def quantize_g(g, half, g_woven):
            cols = slice((half + 1) * HALF, (half + 2) * HALF)
            nc.vector.quantize_mx(
                g_codes[g][:, cols].bitcast(E5M2), g_scale[g][:, cols], g_woven[:].rearrange("p c t -> p (c t)")
            )

        first_dealt = tile([P, PACK, P, PACK], BF16, "x_dealt", "weight")
        x_cut = X_COLUMNS_ON_SCALAR
        nc.scalar.copy(dealt(first_dealt[:])[:, 0:x_cut], by_row(x_first[:])[:, 0:x_cut])
        nc.vector.tensor_copy(dealt(first_dealt[:])[:, x_cut:P], by_row(x_first[:])[:, x_cut:P])
        quantize_x(0, 0, first_dealt)

        m_rows = xm[0].rearrange("(g p t) d -> g p t d", p=P, t=PACK)
        half_d = D // 2
        m_raw = []
        for u, reuses in enumerate(("w_picked", "w_plane0")):
            m_half = tile([P, ROW_PASSES, PACK, half_d], F32, "m_raw%d" % u, reuses)
            for g in range(ROW_PASSES):
                nc.sync.dma_start(m_half[:, g], m_rows[g][:, :, u * half_d : (u + 1) * half_d])
            m_raw.append(m_half)

        v_codes = tile([P, N], U32, "v_codes", "w_neg")
        nc.vector.tensor_copy(v_codes[:], v_word_table[:].indirect(offsets[:]))
        quantize_x(0, 2, first_dealt, "w_plane1")

        second_dealt = tile([P, PACK, P, PACK], BF16, "x_dealt1")
        for u, copy in enumerate((nc.scalar.copy, nc.vector.tensor_copy)):
            copy(dealt(second_dealt[:])[:, u * (P // 2) : (u + 1) * (P // 2)], by_row(x_second[u][:]))
        for t in range(0, PACK, 2):
            quantize_x(1, t, second_dealt)

        weighted_first = tile([P, PACK, N], F32, "weighted_first", "w_plane2")
        g_first = tile([P, PACK, N], BF16, "g_first", "x_dealt1")
        for group in ((0, 1), (2,), (3,)):
            banks = {t: score_psum.tile([P, N], F32, name="first_bank%d" % t) for t in group}
            for t in group:
                score_pass(banks[t], 0, t, w_codes[:], w_scale[:], True)
            for t in group:
                score_pass(banks[t], 0, t, v_codes[:], v_scale[:], False)
            for t in group:
                weigh_and_clip(banks[t], 0, t, weighted_first, g_first)

        def weave_g(name, planes, copy, reuses=None):
            g_woven = tile([P, HALF, PACK], BF16, name, reuses)
            copy(woven(g_woven[:]), planar(planes))
            return g_woven

        def second_pass(half, bank_names):
            slots = slice(half * HALF, (half + 1) * HALF)
            weighted = tile([P, PACK, HALF], F32, "weighted_second%d" % half)
            g_planes = tile([P, PACK, HALF], BF16, "g_second%d" % half)
            for t in range(PACK):
                bank = score_psum.tile([P, HALF], F32, name=bank_names[t])
                score_pass(bank, 1, t, w_codes[:, slots], w_scale[:, slots], True)
                score_pass(bank, 1, t, v_codes[:, slots], v_scale[:, slots], False)
                weigh_and_clip(bank, 1, t, weighted, g_planes)
            return g_planes

        m_codes = [tile([P, ROW_PASSES * P], U32, "m_codes%d" % k) for k in range(D_TILES)]
        m_scale = [tile([P, ROW_PASSES * P], U8, "m_scale%d" % k) for k in range(D_TILES)]

        def quantize_m(k, reuses):
            m_woven = tile([P, ROW_PASSES, P, PACK], BF16, "m_woven%d" % k, reuses)
            for g in range(ROW_PASSES):
                nc.scalar.copy(woven(m_woven[:, g]), planar(m_raw[k // 2][:, g, :, k % 2 * P : (k % 2 + 1) * P]))
            source = m_woven[:].rearrange("p g c t -> p (g c t)")
            nc.vector.quantize_mx(m_codes[k][:].bitcast(E4M3), m_scale[k][:], source)

        def gradient_passes(k, first_column):
            bank = grad_psum.tile([P, N], F32, name="grad_bank")
            moving = slice(first_column, first_column + N)
            for g in range(ROW_PASSES):
                cols = slice(g * P, (g + 1) * P)
                nc.tensor.matmul_mx(
                    bank[:],
                    lhsT=m_codes[k][:, cols].bitcast(E4M3),
                    lhsT_scale=m_scale[k][:, cols],
                    rhs=g_codes[g][:, moving].bitcast(E5M2),
                    rhs_scale=g_scale[g][:, moving],
                    start=(g == 0),
                    stop=(g == ROW_PASSES - 1),
                )
            return bank

        first_low = weave_g("first_low", g_first[:, :, 0:HALF], nc.vector.tensor_copy)
        second_low_planes = second_pass(0, ("second_bank0", "second_bank1", "first_bank0", "first_bank1"))
        quantize_g(0, 0, first_low)
        second_low = weave_g("second_low", second_low_planes[:], nc.vector.tensor_copy)
        quantize_m(0, "w_plane2")
        quantize_g(1, 0, second_low)
        low_bank = gradient_passes(0, 0)

        second_high_planes = second_pass(1, ("first_bank2", "first_bank3", "second_bank0", "second_bank1"))
        first_high = weave_g("first_high", g_first[:, :, HALF:N], nc.scalar.copy, "neg_weight")
        second_high = weave_g("second_high", second_high_planes[:], nc.vector.tensor_copy)
        quantize_g(0, 1, first_high)
        quantize_g(1, 1, second_high)

        grad_low = tile([P, HALF], F32, "grad_low", "weighted_second1")
        nc.scalar.copy(grad_low[:], low_bank[:, HALF:N])
        nc.vector.tensor_copy(windows[0][:].indirect(offsets[:, 0 : HALF // PER_COLUMN]), grad_low[:])

        for k in range(D_TILES):
            bank = gradient_passes(k, HALF)
            if k + 1 < D_TILES:
                quantize_m(k + 1, "upper" if k == 0 else "m_codes%d" % (k - 1))
            first_slot = HALF if k == 0 else 0
            grad = tile([P, N - first_slot], F32, "grad%d" % k)
            nc.scalar.copy(grad[:], bank[:, first_slot:N])
            slots_left = offsets[:, first_slot // PER_COLUMN : N // PER_COLUMN]
            nc.vector.tensor_copy(windows[k][:].indirect(slots_left), grad[:])
            nc.sync.dma_start(out[k * P : (k + 1) * P, :], windows[k][:])
